import numpy as np
import ml_dtypes


def mxq(x, axis, fmt="e4m3"):
    dtype, down = {"e4m3": (ml_dtypes.float8_e4m3fn, 7), "e5m2": (ml_dtypes.float8_e5m2, 14)}[fmt]
    v = np.moveaxis(np.asarray(x, np.float32).astype(ml_dtypes.bfloat16).astype(np.float64), axis, -1)
    blocks = v.reshape(v.shape[:-1] + (-1, 32))
    amax = np.abs(blocks).max(-1, keepdims=True)
    byte = np.maximum(np.where(amax > 0, np.frexp(amax)[1] - 1 + 127, 0) - down, 1)
    scale = np.exp2(byte - 127.0)
    codes = (blocks / scale).astype(np.float32).astype(dtype).astype(np.float64)
    return np.moveaxis((codes * scale).reshape(v.shape), -1, axis)


WIDE = False


def mx_kscale(k):
    if not WIDE:
        return np.ones(k)
    levels = np.array([10, -10, 5, -5, 0])
    if k % 512:
        return np.exp2(np.random.permutation(np.resize(levels, k // 32))).repeat(32)
    a = np.empty((k // 512, 16))
    for p in range(k // 512):
        a[p, :8] = np.random.permutation(np.resize(levels, 8))
        for g in range(8):
            far = levels[np.abs(levels - a[p, g]) >= 10]
            a[p, g + 8] = far[np.random.randint(len(far))]
    return np.exp2(a.ravel()).repeat(32)


def f64(x):
    return np.asarray(x).astype(np.float64)


def striped(idx):
    return np.tile(np.asarray(idx).reshape(-1, 16).T, (8, 1)).astype(np.uint16)


def unstriped(offs):
    return offs[:16].T.reshape(-1).astype(np.int64)


E2M1 = np.array([0.0, 0.5, 1.0, 1.5, 2.0, 3.0, 4.0, 6.0, -0.0, -0.5, -1.0, -1.5, -2.0, -3.0, -4.0, -6.0])


def pack_weight(w, fmt):
    k, n = w.shape
    w = f64(np.asarray(w, np.float32).astype(ml_dtypes.bfloat16)).reshape(k // 32, 32, n)
    amax = np.abs(w).max(1)
    if fmt == "e4m3":
        byte = np.frexp(amax)[1] - 1 + 127 - 7
    else:
        mant, ex = np.frexp(amax / 6.0)
        byte = np.where(mant > 0.5, ex, ex - 1) + 127
    byte = np.clip(np.where(amax > 0, byte, 1), 1, 254)
    scaled = (w * np.exp2(127.0 - byte)[:, None, :]).reshape(k, n).astype(np.float32)
    by_word = np.ascontiguousarray(scaled.reshape(k // 512, 128, 4, n).transpose(0, 1, 3, 2))
    if fmt == "e4m3":
        words = by_word.astype(ml_dtypes.float8_e4m3fn).view(np.uint8)
    else:
        c = by_word.astype(ml_dtypes.float4_e2m1fn).view(np.uint8) & 0xF
        words = (c[..., 0::2] | (c[..., 1::2] << 4)).reshape(k // 512, 128, 2 * n)
    return np.ascontiguousarray(words), np.ascontiguousarray(byte.astype(np.uint8).reshape(k // 512, 16, n))


def unpack_weight(words, scales, fmt):
    g, _, n = scales.shape
    words = np.ascontiguousarray(words).reshape(g, 128, n, -1)
    if fmt == "e4m3":
        vals = words.view(ml_dtypes.float8_e4m3fn).astype(np.float64)
    else:
        nib = np.empty((g, 128, n, 4), np.uint8)
        nib[..., 0::2] = words & 0xF
        nib[..., 1::2] = words >> 4
        vals = E2M1[nib]
    vals = vals * np.repeat(np.exp2(scales.astype(np.float64) - 127.0), 8, axis=1)[..., None]
    return vals.transpose(0, 1, 3, 2).reshape(g * 512, n)


D, E, T, I, Q = 512, 512, 2048, 512, 128


def setup_inputs():
    n = np.random.standard_normal
    idx = np.random.permutation(T)[:I]
    fd = mx_kscale(D)
    fe = mx_kscale(E)
    keysp = pack_weight(n((D, T)) / fd[:, None], "e2m1")
    valsp = pack_weight(n((E, T)) / fe[:, None], "e2m1")
    return {
        "query": (n((D, Q)) * 0.4 / np.sqrt(D) * fd[:, None]).astype(np.float32),
        "query2": (n((D, Q)) * 0.5 / np.sqrt(D) * fd[:, None]).astype(np.float32),
        "keys_words": keysp[0],
        "keys_scales": keysp[1],
        "gout": (n((E, Q)) * 1 / np.sqrt(E) * fe[:, None]).astype(np.float32),
        "vals_words": valsp[0],
        "vals_scales": valsp[1],
        "size": (np.random.uniform(0.5, 2.0, (1, I))).astype(np.float32),
        "dquery": (n((D, Q)) * 1.0 / np.sqrt(D) * fd[:, None]).astype(np.float32),
        "base": (0.5 * n((Q, T))).astype(np.float32),
        "offs": striped(idx),
    }


def reference(query, query2, keys_words, keys_scales, gout, vals_words, vals_scales, size, dquery, base, offs):
    idx = unstriped(offs)
    keysu = unpack_weight(keys_words, keys_scales, "e2m1")
    valsu = unpack_weight(vals_words, vals_scales, "e2m1")
    queryq = mxq(f64(query), 0, "e4m3")
    keysidxg = keysu[:, idx]
    a = queryq.T @ keysidxg
    dqueryq = mxq(f64(dquery), 0, "e4m3")
    ta = dqueryq.T @ keysidxg
    query2q = mxq(f64(query2), 0, "e4m3")
    b = query2q.T @ keysidxg
    s = a * (b + 1.0)
    p = np.exp(s - np.max(s, axis=1, keepdims=True))
    z = np.sum(p, axis=1, keepdims=True)
    goutq = mxq(f64(gout), 0, "e4m3")
    valsidxg = valsu[:, idx]
    c0 = goutq.T @ valsidxg
    dz = np.sum(c0 * p * f64(size) / np.square(z) * (-1.0), axis=1, keepdims=True)
    dp = c0 / z * f64(size) + dz
    ts = ta * (b + 1.0)
    tp = ts * p
    tz = np.sum(tp, axis=1, keepdims=True)
    tdz = np.sum((tp * f64(size) * c0 - tz * z * 2.0 * c0 * p * f64(size) / np.square(z)) / np.square(z) * (-1.0), axis=1, keepdims=True)
    tdp = tz * c0 / np.square(z) * (-1.0) * f64(size) + tdz
    tds = tdp * p + tp * dp
    tda = tds * (b + 1.0)
    gs = tda * 512.0
    gf = np.zeros((Q, T))
    gf[:, idx] = gs
    y = f64(base) + gf
    return y

@@ -1,0 +1,197 @@
+from contextlib import ExitStack
+
+import concourse.mybir as mybir
+from concourse.masks import make_identity
+
+D, T, I, Q = 512, 2048, 512, 128
+FLOPS = 4 * 2 * Q * D * I
+
+F32 = mybir.dt.float32
+BF16 = mybir.dt.bfloat16
+I32 = mybir.dt.int32
+U32 = mybir.dt.uint32
+U16 = mybir.dt.uint16
+U8 = mybir.dt.uint8
+FP8X4 = mybir.dt.float8_e4m3fn_x4
+FP4X4 = mybir.dt.float4_e2m1fn_x4
+ALU = mybir.AluOpType
+ACT = mybir.ActivationFunctionType
+
+P = 128
+PACK = 4
+OUT_CHUNKS = (256, 512, 512, 512, 256)
+
+
+def tile_attend_hvproductscore_a_s_kernel(
+    tc, query, query2, keys_words, keys_scales, gout, vals_words, vals_scales, size, dquery, base, offs, out
+):
+    nc = tc.nc
+    with ExitStack() as ctx:
+        sb = ctx.enter_context(tc.tile_pool(name="sb", bufs=1))
+        ps = ctx.enter_context(tc.psum_pool(name="ps", bufs=1))
+
+        def tile(name, shape, dtype, tag=None, bufs=1):
+            return sb.tile(shape, dtype, name=name, tag=tag or name, bufs=bufs, align_bytes=64)
+
+        offsets = tile("offsets", [P, I // 16], U16)
+        pool_words = {"keys": tile("keys_words", [P, T], U16)}
+        pool_scales = {"keys": tile("keys_scales", [P, T], U8, tag="shared"), "vals": tile("vals_scales", [P, T], U8)}
+        words = {n: tile(n + "_gw", [P, I], U16) for n in ("keys", "vals")}
+        scales = {n: tile(n + "_gs", [P, I], U8) for n in ("keys", "vals")}
+        rows = {"query2": query2, "query": query, "dquery": dquery, "gout": gout}
+        raw = {}
+        grouped = {n: tile(n + "_grp", [P, Q, PACK], BF16) for n in rows}
+        codes = {n: tile(n + "_codes", [P, Q], U32) for n in rows}
+        planes = {n: tile(n + "_plane", [P, Q], U8) for n in rows}
+        window = tile("window", [P, T], F32)
+        size_rows = tile("size_rows", [P, P], F32)
+        ident = tile("ident", [P, P], F32)
+        warm = tile("warm", [P, 1], F32, tag="raw", bufs=3)
+
+        def load_scales(name, src, queue):
+            for q in range(4):
+                queue.dma_start(
+                    out=pool_scales[name][32 * q : 32 * q + 4, :].bitcast(I32),
+                    in_=src[0, 4 * q : 4 * q + 4, :].bitcast(I32),
+                )
+
+        def load_words(name, src):
+            nc.sync.dma_start(out=pool_words[name][:].bitcast(I32), in_=src[0].bitcast(I32))
+
+        def load_rows(name):
+            raw[name] = tile(name + "_raw", [P, PACK, Q], F32, tag="raw", bufs=3)
+            nc.sync.dma_start(out=raw[name][:], in_=rows[name].rearrange("(p j) q -> p j q", j=PACK))
+
+        def group(name):
+            nc.scalar.copy(
+                out=grouped[name][:].rearrange("p (c i) t -> p c t i", i=4),
+                in_=raw[name][:].rearrange("p t (c i) -> p c t i", i=4),
+            )
+
+        def quantize(name):
+            nc.vector.quantize_mx(
+                out=codes[name][:].bitcast(FP8X4),
+                scales=planes[name][:],
+                in_=grouped[name][:].rearrange("p c t -> p (c t)"),
+            )
+
+        def gather(dst, src):
+            nc.vector.tensor_copy(dst[:], src[:].indirect(offsets[:]))
+
+        def scores(name):
+            bank = ps.tile([P, I], F32, name=name + "_bank")
+            nc.tensor.matmul_mx(
+                out=bank[:],
+                lhsT=codes[name][:].bitcast(FP8X4),
+                lhsT_scale=planes[name][:],
+                rhs=words["keys"][:].bitcast(FP4X4),
+                rhs_scale=scales["keys"][:],
+                start=True,
+                stop=True,
+            )
+            return bank
+
+        nc.gpsimd.memset(pool_scales["keys"][:].bitcast(I32), 0)
+        nc.vector.memset(pool_scales["vals"][:].bitcast(I32), 0)
+        nc.vector.memset(window[:], 0.0)
+        nc.gpsimd.memset(size_rows[:], 0.0)
+        make_identity(nc, ident[:])
+
+        nc.sync.dma_start(offsets[:], offs)
+        load_scales("keys", keys_scales, nc.scalar)
+        load_words("keys", keys_words)
+        load_rows("query2")
+        load_rows("query")
+        load_scales("vals", vals_scales, nc.sync)
+        nc.scalar.activation(out=warm[:], in_=size_rows[:, 0:1], func=ACT.Exp)
+        load_rows("dquery")
+
+        gather(scales["keys"], pool_scales["keys"])
+        gather(words["keys"], pool_words["keys"])
+        pool_words["vals"] = tile("vals_words", [P, T], U16, tag="shared")
+        load_words("vals", vals_words)
+        group("query2")
+        quantize("query2")
+        b_bank = scores("query2")
+        load_rows("gout")
+        group("query")
+        quantize("query")
+        a_bank = scores("query")
+        nc.sync.dma_start(out=size_rows[0:4, :], in_=size.rearrange("o (j p) -> (o j) p", p=P))
+        group("dquery")
+        quantize("dquery")
+        ta_bank = scores("dquery")
+
+        gather(scales["vals"], pool_scales["vals"])
+        gather(words["vals"], pool_words["vals"])
+        group("gout")
+        quantize("gout")
+        base_sb = tile("base_sb", [P, T], F32, tag="shared")
+        nc.sync.dma_start(out=base_sb[:], in_=base)
+
+        u = tile("u", [P, I], F32)
+        nc.scalar.activation(out=u[:], in_=b_bank[:], func=ACT.Copy, bias=1.0)
+
+        size_bank = ps.tile([P, P], F32, name="size_bank")
+        nc.tensor.transpose(size_bank[:], size_rows[:], ident[:])
+        size_cols = tile("size_cols", [P, 4], F32)
+        nc.scalar.activation(out=size_cols[:], in_=size_bank[:, 0:4], func=ACT.Copy, scale=-512.0)
+
+        s = tile("s", [P, I], F32)
+        neg_max = tile("neg_max", [P, 1], F32)
+        nc.vector.tensor_tensor(s[:], a_bank[:], u[:], ALU.mult)
+        nc.vector.tensor_reduce(neg_max[:], s[:], mybir.AxisListType.X, ALU.max, negate=True)
+        p = tile("p", [P, I], F32)
+        z = tile("z", [P, 1], F32)
+        nc.scalar.activation(out=p[:], in_=s[:], func=ACT.Exp, bias=neg_max[:], accum_out=z[:])
+        ts = tile("ts", [P, I], F32)
+        nc.vector.tensor_tensor(ts[:], ta_bank[:], u[:], ALU.mult)
+
+        c0_banks = [ps.tile([P, 2, Q], F32, name="c0_bank%d" % h) for h in range(2)]
+        c_turned = [tile("c_turned%d" % j, [P, Q], F32) for j in range(4)]
+        c = ps.tile([P, I], F32, name="c_bank")
+        for j in range(4):
+            cols = slice(P * j, P * (j + 1))
+            nc.tensor.matmul_mx(
+                out=c0_banks[j // 2][:, j % 2, :],
+                lhsT=words["vals"][:, cols].bitcast(FP4X4),
+                lhsT_scale=scales["vals"][:, cols],
+                rhs=codes["gout"][:].bitcast(FP8X4),
+                rhs_scale=planes["gout"][:],
+                start=True,
+                stop=True,
+            )
+        for j in range(4):
+            nc.scalar.activation(
+                out=c_turned[j][:], in_=c0_banks[j // 2][:, j % 2, :], func=ACT.Copy, scale=size_cols[:, j : j + 1]
+            )
+        for j in range(4):
+            nc.tensor.transpose(c[:, P * j : P * (j + 1)], c_turned[j][:], ident[:])
+
+        r = tile("r", [P, 1], F32)
+        nc.vector.reciprocal(r[:], z[:])
+        v = tile("v", [P, I], F32)
+        y = tile("y", [P, I], F32)
+        ts_mean = tile("ts_mean", [P, 1], F32)
+        c_mean = tile("c_mean", [P, 1], F32)
+        y_sum = tile("y_sum", [P, 1], F32)
+        nc.vector.scalar_tensor_tensor(v[:], ts[:], r[:], p[:], ALU.mult, ALU.mult, accum_out=ts_mean[:])
+        nc.vector.scalar_tensor_tensor(y[:], c[:], r[:], p[:], ALU.mult, ALU.mult, accum_out=c_mean[:])
+        nc.vector.scalar_tensor_tensor(v[:], ts[:], ts_mean[:], p[:], ALU.subtract, ALU.mult)
+        nc.vector.scalar_tensor_tensor(y[:], c[:], c_mean[:], v[:], ALU.subtract, ALU.mult, accum_out=y_sum[:])
+
+        prob = tile("prob", [P, I], F32)
+        ur = tile("ur", [P, I], F32)
+        nc.scalar.activation(out=prob[:], in_=p[:], func=ACT.Copy, scale=r[:])
+        nc.scalar.activation(out=ur[:], in_=u[:], func=ACT.Copy, scale=r[:])
+        g = tile("g", [P, I], F32)
+        nc.vector.scalar_tensor_tensor(g[:], prob[:], y_sum[:], y[:], ALU.mult, ALU.subtract)
+        nc.vector.tensor_tensor(window[:].indirect(offsets[:]), g[:], ur[:], ALU.mult)
+
+        c0 = 0
+        for n, width in enumerate(OUT_CHUNKS):
+            cols = slice(c0, c0 + width)
+            res = tile("res%d" % n, [P, width], F32)
+            nc.vector.tensor_tensor(res[:], window[:, cols], base_sb[:, cols], ALU.add)
+            nc.sync.dma_start(out=out[:, cols], in_=res[:])
+            c0 += width

@@ -34,32 +34,32 @@ def tile_attend_hvproductscore_a_s_kernel(
             return sb.tile(shape, dtype, name=name, tag=tag or name, bufs=bufs, align_bytes=64)
 
         offsets = tile("offsets", [P, I // 16], U16)
-        pool_words = {"keys": tile("keys_words", [P, T], U16)}
-        pool_scales = {"keys": tile("keys_scales", [P, T], U8, tag="shared"), "vals": tile("vals_scales", [P, T], U8)}
+        pool_words = {n: tile(n + "_words", [P, T], U16, tag="slot_" + n) for n in ("keys", "vals")}
+        pool_scales = {"keys": tile("keys_scales", [P, T], U8, tag="shared"), "vals": tile("vals_scales", [P, T], U8, tag="slot_s")}
         words = {n: tile(n + "_gw", [P, I], U16) for n in ("keys", "vals")}
-        scales = {n: tile(n + "_gs", [P, I], U8) for n in ("keys", "vals")}
+        scales = {"keys": tile("keys_gs", [P, I], U8)}
         rows = {"query2": query2, "query": query, "dquery": dquery, "gout": gout}
         raw = {}
-        grouped = {n: tile(n + "_grp", [P, Q, PACK], BF16) for n in rows}
+        grouped = {n: tile(n + "_grp", [P, Q, PACK], BF16, tag="slot_g" + n) for n in rows}
         codes = {n: tile(n + "_codes", [P, Q], U32) for n in rows}
         planes = {n: tile(n + "_plane", [P, Q], U8) for n in rows}
         window = tile("window", [P, T], F32)
-        size_rows = tile("size_rows", [P, P], F32)
+        size_cols = tile("size_cols", [P, 4], F32)
         ident = tile("ident", [P, P], F32)
-        warm = tile("warm", [P, 1], F32, tag="raw", bufs=3)
+        warm = tile("warm", [P, 1], F32)
 
         def load_scales(name, src, queue):
             for q in range(4):
                 queue.dma_start(
-                    out=pool_scales[name][32 * q : 32 * q + 4, :].bitcast(I32),
-                    in_=src[0, 4 * q : 4 * q + 4, :].bitcast(I32),
+                    out=pool_scales[name][32 * q : 32 * q + 32, :].bitcast(I32),
+                    in_=src[0:1, 4 * q : 4 * q + 4, :].bitcast(I32).broadcast_to([8, 4, T // 4]),
                 )
 
         def load_words(name, src):
             nc.sync.dma_start(out=pool_words[name][:].bitcast(I32), in_=src[0].bitcast(I32))
 
         def load_rows(name):
-            raw[name] = tile(name + "_raw", [P, PACK, Q], F32, tag="raw", bufs=3)
+            raw[name] = tile(name + "_raw", [P, PACK, Q], F32, tag="slot_r" + name)
             nc.sync.dma_start(out=raw[name][:], in_=rows[name].rearrange("(p j) q -> p j q", j=PACK))
 
         def group(name):
@@ -91,85 +91,80 @@ def tile_attend_hvproductscore_a_s_kernel(
             )
             return bank
 
-        nc.gpsimd.memset(pool_scales["keys"][:].bitcast(I32), 0)
-        nc.vector.memset(pool_scales["vals"][:].bitcast(I32), 0)
-        nc.vector.memset(window[:], 0.0)
-        nc.gpsimd.memset(size_rows[:], 0.0)
+        nc.vector.memset(warm[:], 0.0)
+        nc.gpsimd.memset(pool_scales["vals"][:].bitcast(I32), 0)
         make_identity(nc, ident[:])
+        nc.vector.memset(window[:], 0.0)
 
         nc.sync.dma_start(offsets[:], offs)
-        load_scales("keys", keys_scales, nc.scalar)
+        load_scales("keys", keys_scales, nc.sync)
         load_words("keys", keys_words)
         load_rows("query2")
         load_rows("query")
-        load_scales("vals", vals_scales, nc.sync)
-        nc.scalar.activation(out=warm[:], in_=size_rows[:, 0:1], func=ACT.Exp)
+        nc.scalar.activation(out=warm[:], in_=warm[:], func=ACT.Exp)
+        load_words("vals", vals_words)
         load_rows("dquery")
+        load_rows("gout")
+        nc.sync.dma_start(out=size_cols[:], in_=size.rearrange("o (p j) -> (o p) j", j=4))
+        for q in range(4):
+            nc.sync.dma_start(
+                out=pool_scales["vals"][32 * q : 32 * q + 4, :].bitcast(I32),
+                in_=vals_scales[0, 4 * q : 4 * q + 4, :].bitcast(I32),
+            )
 
         gather(scales["keys"], pool_scales["keys"])
         gather(words["keys"], pool_words["keys"])
-        pool_words["vals"] = tile("vals_words", [P, T], U16, tag="shared")
-        load_words("vals", vals_words)
         group("query2")
         quantize("query2")
         b_bank = scores("query2")
-        load_rows("gout")
         group("query")
         quantize("query")
         a_bank = scores("query")
-        nc.sync.dma_start(out=size_rows[0:4, :], in_=size.rearrange("o (j p) -> (o j) p", p=P))
         group("dquery")
         quantize("dquery")
         ta_bank = scores("dquery")
-
-        gather(scales["vals"], pool_scales["vals"])
-        gather(words["vals"], pool_words["vals"])
-        group("gout")
-        quantize("gout")
         base_sb = tile("base_sb", [P, T], F32, tag="shared")
         nc.sync.dma_start(out=base_sb[:], in_=base)
 
         u = tile("u", [P, I], F32)
         nc.scalar.activation(out=u[:], in_=b_bank[:], func=ACT.Copy, bias=1.0)
 
-        size_bank = ps.tile([P, P], F32, name="size_bank")
-        nc.tensor.transpose(size_bank[:], size_rows[:], ident[:])
-        size_cols = tile("size_cols", [P, 4], F32)
-        nc.scalar.activation(out=size_cols[:], in_=size_bank[:, 0:4], func=ACT.Copy, scale=-512.0)
-
-        s = tile("s", [P, I], F32)
-        neg_max = tile("neg_max", [P, 1], F32)
+        group("gout")
+        s = tile("s", [P, I], F32, tag="slot_score")
         nc.vector.tensor_tensor(s[:], a_bank[:], u[:], ALU.mult)
+        gather(words["vals"], pool_words["vals"])
+        neg_max = tile("neg_max", [P, 1], F32, tag="slot_vals")
         nc.vector.tensor_reduce(neg_max[:], s[:], mybir.AxisListType.X, ALU.max, negate=True)
-        p = tile("p", [P, I], F32)
+        p = tile("p", [P, I], F32, tag="slot_rgout")
         z = tile("z", [P, 1], F32)
         nc.scalar.activation(out=p[:], in_=s[:], func=ACT.Exp, bias=neg_max[:], accum_out=z[:])
-        ts = tile("ts", [P, I], F32)
-        nc.vector.tensor_tensor(ts[:], ta_bank[:], u[:], ALU.mult)
-
-        c0_banks = [ps.tile([P, 2, Q], F32, name="c0_bank%d" % h) for h in range(2)]
-        c_turned = [tile("c_turned%d" % j, [P, Q], F32) for j in range(4)]
-        c = ps.tile([P, I], F32, name="c_bank")
+        quantize("gout")
+        scales["vals"] = tile("vals_gs", [P, I], U8, tag="slot_ggout")
+        gather(scales["vals"], pool_scales["vals"])
+        c0_bank = ps.tile([P, I], F32, name="c0_bank")
+        nc.tensor.matmul_mx(
+            out=c0_bank[:],
+            lhsT=codes["gout"][:].bitcast(FP8X4),
+            lhsT_scale=planes["gout"][:],
+            rhs=words["vals"][:].bitcast(FP4X4),
+            rhs_scale=scales["vals"][:],
+            start=True,
+            stop=True,
+        )
+        size_bank = ps.tile([P, 4, P], F32, name="size_bank")
         for j in range(4):
-            cols = slice(P * j, P * (j + 1))
-            nc.tensor.matmul_mx(
-                out=c0_banks[j // 2][:, j % 2, :],
-                lhsT=words["vals"][:, cols].bitcast(FP4X4),
-                lhsT_scale=scales["vals"][:, cols],
-                rhs=codes["gout"][:].bitcast(FP8X4),
-                rhs_scale=planes["gout"][:],
-                start=True,
-                stop=True,
-            )
-        for j in range(4):
-            nc.scalar.activation(
-                out=c_turned[j][:], in_=c0_banks[j // 2][:, j % 2, :], func=ACT.Copy, scale=size_cols[:, j : j + 1]
-            )
-        for j in range(4):
-            nc.tensor.transpose(c[:, P * j : P * (j + 1)], c_turned[j][:], ident[:])
+            nc.tensor.transpose(size_bank[:, j, :], size_cols[:, j : j + 1].to_broadcast([P, P]), ident[:])
+        size_all = tile("size_all", [P, P, 4], F32, tag="slot_score")
+        nc.scalar.activation(
+            out=size_all[:], in_=size_bank[:].rearrange("m j p -> m p j"), func=ACT.Copy, scale=-512.0
+        )
 
         r = tile("r", [P, 1], F32)
         nc.vector.reciprocal(r[:], z[:])
+        ts = tile("ts", [P, I], F32, tag="slot_s")
+        nc.vector.tensor_tensor(ts[:], ta_bank[:], u[:], ALU.mult)
+        c = tile("c", [P, I], F32)
+        nc.vector.tensor_tensor(c[:], c0_bank[:], size_all[:].rearrange("m p j -> m (p j)"), ALU.mult)
         v = tile("v", [P, I], F32)
         y = tile("y", [P, I], F32)
         ts_mean = tile("ts_mean", [P, 1], F32)

@@ -102,8 +102,8 @@ def tile_attend_hvproductscore_a_s_kernel(
         load_rows("query2")
         load_rows("query")
         nc.scalar.activation(out=warm[:], in_=warm[:], func=ACT.Exp)
-        load_words("vals", vals_words)
         load_rows("dquery")
+        load_words("vals", vals_words)
         load_rows("gout")
         nc.sync.dma_start(out=size_cols[:], in_=size.rearrange("o (p j) -> (o p) j", j=4))
         for q in range(4):
@@ -129,6 +129,10 @@ def tile_attend_hvproductscore_a_s_kernel(
         u = tile("u", [P, I], F32)
         nc.scalar.activation(out=u[:], in_=b_bank[:], func=ACT.Copy, bias=1.0)
 
+        ta = tile("ta", [P, I], F32)
+        ts = tile("ts", [P, I], F32)
+        nc.scalar.copy(out=ta[:], in_=ta_bank[:])
+        nc.gpsimd.tensor_tensor(ts[:], ta[:], u[:], ALU.mult)
         group("gout")
         s = tile("s", [P, I], F32, tag="slot_score")
         nc.vector.tensor_tensor(s[:], a_bank[:], u[:], ALU.mult)
@@ -159,10 +163,8 @@ def tile_attend_hvproductscore_a_s_kernel(
             out=size_all[:], in_=size_bank[:].rearrange("m j p -> m p j"), func=ACT.Copy, scale=-512.0
         )
 
-        r = tile("r", [P, 1], F32)
+        r = tile("r", [P, 1], F32, tag="slot_s")
         nc.vector.reciprocal(r[:], z[:])
-        ts = tile("ts", [P, I], F32, tag="slot_s")
-        nc.vector.tensor_tensor(ts[:], ta_bank[:], u[:], ALU.mult)
         c = tile("c", [P, I], F32)
         nc.vector.tensor_tensor(c[:], c0_bank[:], size_all[:].rearrange("m p j -> m (p j)"), ALU.mult)
         v = tile("v", [P, I], F32)

@@ -19,7 +19,13 @@ ACT = mybir.ActivationFunctionType
 
 P = 128
 PACK = 4
-OUT_CHUNKS = (256, 512, 512, 512, 256)
+QUADRANTS = 4
+QUADRANT = P // QUADRANTS
+SCALE_ROWS = 4
+LINE = 4
+SIZES_A_PARTITION = I // P
+OUT_SCALE = 512.0
+OUT_PIECES = (256, 512, 512, 512, 256)
 
 
 def tile_attend_hvproductscore_a_s_kernel(
@@ -30,100 +36,106 @@ def tile_attend_hvproductscore_a_s_kernel(
         sb = ctx.enter_context(tc.tile_pool(name="sb", bufs=1))
         ps = ctx.enter_context(tc.psum_pool(name="ps", bufs=1))
 
-        def tile(name, shape, dtype, tag=None, bufs=1):
-            return sb.tile(shape, dtype, name=name, tag=tag or name, bufs=bufs, align_bytes=64)
+        def tile(name, shape, dtype, tag=None):
+            return sb.tile(shape, dtype, name=name, tag=tag or name, bufs=1, align_bytes=64)
 
         offsets = tile("offsets", [P, I // 16], U16)
-        pool_words = {n: tile(n + "_words", [P, T], U16, tag="slot_" + n) for n in ("keys", "vals")}
-        pool_scales = {"keys": tile("keys_scales", [P, T], U8, tag="shared"), "vals": tile("vals_scales", [P, T], U8, tag="slot_s")}
-        words = {n: tile(n + "_gw", [P, I], U16) for n in ("keys", "vals")}
-        scales = {"keys": tile("keys_gs", [P, I], U8)}
+        pool_words = {
+            "keys": tile("keys_words", [P, T], U16),
+            "vals": tile("vals_words", [P, T], U16, tag="vals_words_then_neg_max"),
+        }
+        pool_scales = {
+            "keys": tile("keys_scales", [P, T], U8, tag="keys_scales_then_base"),
+            "vals": tile("vals_scales", [P, T], U8, tag="vals_scales_then_v"),
+        }
+        listed_words = {n: tile(n + "_listed_words", [P, I], U16) for n in ("keys", "vals")}
+        listed_scales = {n: tile(n + "_listed_scales", [P, I], U8) for n in ("keys", "vals")}
         rows = {"query2": query2, "query": query, "dquery": dquery, "gout": gout}
-        raw = {}
-        grouped = {n: tile(n + "_grp", [P, Q, PACK], BF16, tag="slot_g" + n) for n in rows}
+        raw = {n: tile(n + "_raw", [P, PACK, Q], F32) for n in ("query2", "query", "dquery")}
+        raw["gout"] = tile("gout_raw", [P, PACK, Q], F32, tag="gout_raw_then_p")
+        grouped = {n: tile(n + "_grouped", [P, Q, PACK], BF16) for n in rows}
         codes = {n: tile(n + "_codes", [P, Q], U32) for n in rows}
-        planes = {n: tile(n + "_plane", [P, Q], U8) for n in rows}
+        code_scales = {n: tile(n + "_code_scales", [P, Q], U8) for n in rows}
         window = tile("window", [P, T], F32)
-        size_cols = tile("size_cols", [P, 4], F32)
+        size_cols = tile("size_cols", [P, SIZES_A_PARTITION], F32)
         ident = tile("ident", [P, P], F32)
-        warm = tile("warm", [P, 1], F32)
-
-        def load_scales(name, src, queue):
-            for q in range(4):
-                queue.dma_start(
-                    out=pool_scales[name][32 * q : 32 * q + 32, :].bitcast(I32),
-                    in_=src[0:1, 4 * q : 4 * q + 4, :].bitcast(I32).broadcast_to([8, 4, T // 4]),
-                )
+        minus_one = tile("minus_one", [P, 1], F32)
 
         def load_words(name, src):
             nc.sync.dma_start(out=pool_words[name][:].bitcast(I32), in_=src[0].bitcast(I32))
 
         def load_rows(name):
-            raw[name] = tile(name + "_raw", [P, PACK, Q], F32, tag="slot_r" + name)
-            nc.sync.dma_start(out=raw[name][:], in_=rows[name].rearrange("(p j) q -> p j q", j=PACK))
+            nc.sync.dma_start(out=raw[name][:], in_=rows[name].rearrange("(p t) q -> p t q", t=PACK))
 
         def group(name):
-            nc.scalar.copy(
-                out=grouped[name][:].rearrange("p (c i) t -> p c t i", i=4),
-                in_=raw[name][:].rearrange("p t (c i) -> p c t i", i=4),
+            nc.scalar.activation(
+                out=grouped[name][:].rearrange("p (c i) t -> p c t i", i=LINE),
+                in_=raw[name][:].rearrange("p t (c i) -> p c t i", i=LINE),
+                func=ACT.Copy,
             )
 
         def quantize(name):
             nc.vector.quantize_mx(
                 out=codes[name][:].bitcast(FP8X4),
-                scales=planes[name][:],
+                scales=code_scales[name][:],
                 in_=grouped[name][:].rearrange("p c t -> p (c t)"),
             )
 
-        def gather(dst, src):
-            nc.vector.tensor_copy(dst[:], src[:].indirect(offsets[:]))
+        def gather(listed, pool):
+            nc.vector.tensor_copy(listed[:], pool[:].indirect(offsets[:]))
 
-        def scores(name):
+        def product(name, pool_name):
             bank = ps.tile([P, I], F32, name=name + "_bank")
             nc.tensor.matmul_mx(
                 out=bank[:],
                 lhsT=codes[name][:].bitcast(FP8X4),
-                lhsT_scale=planes[name][:],
-                rhs=words["keys"][:].bitcast(FP4X4),
-                rhs_scale=scales["keys"][:],
+                lhsT_scale=code_scales[name][:],
+                rhs=listed_words[pool_name][:].bitcast(FP4X4),
+                rhs_scale=listed_scales[pool_name][:],
                 start=True,
                 stop=True,
             )
             return bank
 
-        nc.vector.memset(warm[:], 0.0)
         nc.gpsimd.memset(pool_scales["vals"][:].bitcast(I32), 0)
         make_identity(nc, ident[:])
+        nc.gpsimd.memset(minus_one[:], -1.0)
         nc.vector.memset(window[:], 0.0)
 
         nc.sync.dma_start(offsets[:], offs)
-        load_scales("keys", keys_scales, nc.sync)
+        for q in range(QUADRANTS):
+            nc.sync.dma_start(
+                out=pool_scales["keys"][QUADRANT * q : QUADRANT * (q + 1), :].bitcast(I32),
+                in_=keys_scales[0:1, SCALE_ROWS * q : SCALE_ROWS * (q + 1), :]
+                .bitcast(I32)
+                .broadcast_to([QUADRANT // SCALE_ROWS, SCALE_ROWS, T // 4]),
+            )
         load_words("keys", keys_words)
         load_rows("query2")
         load_rows("query")
-        nc.scalar.activation(out=warm[:], in_=warm[:], func=ACT.Exp)
         load_rows("dquery")
         load_words("vals", vals_words)
         load_rows("gout")
-        nc.sync.dma_start(out=size_cols[:], in_=size.rearrange("o (p j) -> (o p) j", j=4))
-        for q in range(4):
+        nc.sync.dma_start(out=size_cols[:], in_=size.rearrange("o (p j) -> (o p) j", j=SIZES_A_PARTITION))
+        for q in range(QUADRANTS):
             nc.sync.dma_start(
-                out=pool_scales["vals"][32 * q : 32 * q + 4, :].bitcast(I32),
-                in_=vals_scales[0, 4 * q : 4 * q + 4, :].bitcast(I32),
+                out=pool_scales["vals"][QUADRANT * q : QUADRANT * q + SCALE_ROWS, :].bitcast(I32),
+                in_=vals_scales[0, SCALE_ROWS * q : SCALE_ROWS * (q + 1), :].bitcast(I32),
             )
 
-        gather(scales["keys"], pool_scales["keys"])
-        gather(words["keys"], pool_words["keys"])
+        gather(listed_scales["keys"], pool_scales["keys"])
+        gather(listed_words["keys"], pool_words["keys"])
         group("query2")
         quantize("query2")
-        b_bank = scores("query2")
+        b_bank = product("query2", "keys")
         group("query")
         quantize("query")
-        a_bank = scores("query")
+        a_bank = product("query", "keys")
         group("dquery")
         quantize("dquery")
-        ta_bank = scores("dquery")
-        base_sb = tile("base_sb", [P, T], F32, tag="shared")
+        ta_bank = product("dquery", "keys")
+
+        base_sb = tile("base_sb", [P, T], F32, tag="keys_scales_then_base")
         nc.sync.dma_start(out=base_sb[:], in_=base)
 
         u = tile("u", [P, I], F32)
@@ -134,61 +146,54 @@ def tile_attend_hvproductscore_a_s_kernel(
         nc.scalar.copy(out=ta[:], in_=ta_bank[:])
         nc.gpsimd.tensor_tensor(ts[:], ta[:], u[:], ALU.mult)
         group("gout")
-        s = tile("s", [P, I], F32, tag="slot_score")
+
+        s = tile("s", [P, I], F32, tag="s_then_size_all")
         nc.vector.tensor_tensor(s[:], a_bank[:], u[:], ALU.mult)
-        gather(words["vals"], pool_words["vals"])
-        neg_max = tile("neg_max", [P, 1], F32, tag="slot_vals")
+        gather(listed_words["vals"], pool_words["vals"])
+        quantize("gout")
+        neg_max = tile("neg_max", [P, 1], F32, tag="vals_words_then_neg_max")
         nc.vector.tensor_reduce(neg_max[:], s[:], mybir.AxisListType.X, ALU.max, negate=True)
-        p = tile("p", [P, I], F32, tag="slot_rgout")
+        p = tile("p", [P, I], F32, tag="gout_raw_then_p")
         z = tile("z", [P, 1], F32)
         nc.scalar.activation(out=p[:], in_=s[:], func=ACT.Exp, bias=neg_max[:], accum_out=z[:])
-        quantize("gout")
-        scales["vals"] = tile("vals_gs", [P, I], U8, tag="slot_ggout")
-        gather(scales["vals"], pool_scales["vals"])
-        c0_bank = ps.tile([P, I], F32, name="c0_bank")
-        nc.tensor.matmul_mx(
-            out=c0_bank[:],
-            lhsT=codes["gout"][:].bitcast(FP8X4),
-            lhsT_scale=planes["gout"][:],
-            rhs=words["vals"][:].bitcast(FP4X4),
-            rhs_scale=scales["vals"][:],
-            start=True,
-            stop=True,
-        )
-        size_bank = ps.tile([P, 4, P], F32, name="size_bank")
-        for j in range(4):
+        gather(listed_scales["vals"], pool_scales["vals"])
+        c0_bank = product("gout", "vals")
+
+        size_bank = ps.tile([P, SIZES_A_PARTITION, P], F32, name="size_bank")
+        for j in range(SIZES_A_PARTITION):
             nc.tensor.transpose(size_bank[:, j, :], size_cols[:, j : j + 1].to_broadcast([P, P]), ident[:])
-        size_all = tile("size_all", [P, P, 4], F32, tag="slot_score")
+        size_all = tile("size_all", [P, P, SIZES_A_PARTITION], F32, tag="s_then_size_all")
         nc.scalar.activation(
-            out=size_all[:], in_=size_bank[:].rearrange("m j p -> m p j"), func=ACT.Copy, scale=-512.0
+            out=size_all[:], in_=size_bank[:].rearrange("m j n -> m n j"), func=ACT.Copy, scale=-OUT_SCALE
         )
 
-        r = tile("r", [P, 1], F32, tag="slot_s")
-        nc.vector.reciprocal(r[:], z[:])
-        c = tile("c", [P, I], F32)
-        nc.vector.tensor_tensor(c[:], c0_bank[:], size_all[:].rearrange("m p j -> m (p j)"), ALU.mult)
-        v = tile("v", [P, I], F32)
-        y = tile("y", [P, I], F32)
+        r = tile("r", [P, 1], F32)
+        nc.gpsimd.tensor_tensor(r[:], z[:], minus_one[:], ALU.pow)
+
         ts_mean = tile("ts_mean", [P, 1], F32)
         c_mean = tile("c_mean", [P, 1], F32)
         y_sum = tile("y_sum", [P, 1], F32)
+        v = tile("v", [P, I], F32, tag="vals_scales_then_v")
         nc.vector.scalar_tensor_tensor(v[:], ts[:], r[:], p[:], ALU.mult, ALU.mult, accum_out=ts_mean[:])
-        nc.vector.scalar_tensor_tensor(y[:], c[:], r[:], p[:], ALU.mult, ALU.mult, accum_out=c_mean[:])
+        c = tile("c", [P, I], F32)
+        nc.vector.tensor_tensor(c[:], c0_bank[:], size_all[:].rearrange("m n j -> m (n j)"), ALU.mult)
         nc.vector.scalar_tensor_tensor(v[:], ts[:], ts_mean[:], p[:], ALU.subtract, ALU.mult)
+        y = tile("y", [P, I], F32)
+        nc.vector.scalar_tensor_tensor(y[:], c[:], r[:], p[:], ALU.mult, ALU.mult, accum_out=c_mean[:])
         nc.vector.scalar_tensor_tensor(y[:], c[:], c_mean[:], v[:], ALU.subtract, ALU.mult, accum_out=y_sum[:])
 
-        prob = tile("prob", [P, I], F32)
+        pr = tile("pr", [P, I], F32)
         ur = tile("ur", [P, I], F32)
-        nc.scalar.activation(out=prob[:], in_=p[:], func=ACT.Copy, scale=r[:])
+        nc.scalar.activation(out=pr[:], in_=p[:], func=ACT.Copy, scale=r[:])
         nc.scalar.activation(out=ur[:], in_=u[:], func=ACT.Copy, scale=r[:])
-        g = tile("g", [P, I], F32)
-        nc.vector.scalar_tensor_tensor(g[:], prob[:], y_sum[:], y[:], ALU.mult, ALU.subtract)
-        nc.vector.tensor_tensor(window[:].indirect(offsets[:]), g[:], ur[:], ALU.mult)
+        centred = tile("centred", [P, I], F32)
+        nc.vector.scalar_tensor_tensor(centred[:], pr[:], y_sum[:], y[:], ALU.mult, ALU.subtract)
+        nc.vector.tensor_tensor(window[:].indirect(offsets[:]), centred[:], ur[:], ALU.mult)
 
-        c0 = 0
-        for n, width in enumerate(OUT_CHUNKS):
-            cols = slice(c0, c0 + width)
-            res = tile("res%d" % n, [P, width], F32)
-            nc.vector.tensor_tensor(res[:], window[:, cols], base_sb[:, cols], ALU.add)
-            nc.sync.dma_start(out=out[:, cols], in_=res[:])
-            c0 += width
+        first = 0
+        for n, width in enumerate(OUT_PIECES):
+            cols = slice(first, first + width)
+            piece = tile("piece%d" % n, [P, width], F32)
+            nc.vector.tensor_tensor(piece[:], window[:, cols], base_sb[:, cols], ALU.add)
+            nc.sync.dma_start(out=out[:, cols], in_=piece[:])
+            first += width

@@ -60,6 +60,7 @@ def tile_attend_hvproductscore_a_s_kernel(
         size_cols = tile("size_cols", [P, SIZES_A_PARTITION], F32)
         ident = tile("ident", [P, P], F32)
         minus_one = tile("minus_one", [P, 1], F32)
+        warm = tile("warm", [P, 1], F32)
 
         def load_words(name, src):
             nc.sync.dma_start(out=pool_words[name][:].bitcast(I32), in_=src[0].bitcast(I32))
@@ -68,10 +69,9 @@ def tile_attend_hvproductscore_a_s_kernel(
             nc.sync.dma_start(out=raw[name][:], in_=rows[name].rearrange("(p t) q -> p t q", t=PACK))
 
         def group(name):
-            nc.scalar.activation(
+            nc.scalar.copy(
                 out=grouped[name][:].rearrange("p (c i) t -> p c t i", i=LINE),
                 in_=raw[name][:].rearrange("p t (c i) -> p c t i", i=LINE),
-                func=ACT.Copy,
             )
 
         def quantize(name):
@@ -97,6 +97,7 @@ def tile_attend_hvproductscore_a_s_kernel(
             )
             return bank
 
+        nc.vector.memset(warm[:], 0.0)
         nc.gpsimd.memset(pool_scales["vals"][:].bitcast(I32), 0)
         make_identity(nc, ident[:])
         nc.gpsimd.memset(minus_one[:], -1.0)
@@ -113,6 +114,7 @@ def tile_attend_hvproductscore_a_s_kernel(
         load_words("keys", keys_words)
         load_rows("query2")
         load_rows("query")
+        nc.scalar.activation(out=warm[:], in_=warm[:], func=ACT.Exp)
         load_rows("dquery")
         load_words("vals", vals_words)
         load_rows("gout")

from contextlib import ExitStack

import concourse.mybir as mybir
from concourse.masks import make_identity

D, T, I, Q = 512, 2048, 512, 128
FLOPS = 4 * 2 * Q * D * I

F32 = mybir.dt.float32
BF16 = mybir.dt.bfloat16
I32 = mybir.dt.int32
U32 = mybir.dt.uint32
U16 = mybir.dt.uint16
U8 = mybir.dt.uint8
FP8X4 = mybir.dt.float8_e4m3fn_x4
FP4X4 = mybir.dt.float4_e2m1fn_x4
ALU = mybir.AluOpType
ACT = mybir.ActivationFunctionType

P = 128
PACK = 4
QUADRANTS = 4
QUADRANT = P // QUADRANTS
SCALE_ROWS = 4
LINE = 4
SIZES_A_PARTITION = I // P
OUT_SCALE = 512.0
OUT_PIECES = (256, 512, 512, 512, 256)


def tile_attend_hvproductscore_a_s_kernel(
    tc, query, query2, keys_words, keys_scales, gout, vals_words, vals_scales, size, dquery, base, offs, out
):
    nc = tc.nc
    with ExitStack() as ctx:
        sb = ctx.enter_context(tc.tile_pool(name="sb", bufs=1))
        ps = ctx.enter_context(tc.psum_pool(name="ps", bufs=1))

        def tile(name, shape, dtype, tag=None):
            return sb.tile(shape, dtype, name=name, tag=tag or name, bufs=1, align_bytes=64)

        offsets = tile("offsets", [P, I // 16], U16)
        pool_words = {
            "keys": tile("keys_words", [P, T], U16),
            "vals": tile("vals_words", [P, T], U16, tag="vals_words_then_neg_max"),
        }
        pool_scales = {
            "keys": tile("keys_scales", [P, T], U8, tag="keys_scales_then_base"),
            "vals": tile("vals_scales", [P, T], U8, tag="vals_scales_then_v"),
        }
        listed_words = {n: tile(n + "_listed_words", [P, I], U16) for n in ("keys", "vals")}
        listed_scales = {n: tile(n + "_listed_scales", [P, I], U8) for n in ("keys", "vals")}
        rows = {"query2": query2, "query": query, "dquery": dquery, "gout": gout}
        raw = {n: tile(n + "_raw", [P, PACK, Q], F32) for n in ("query2", "query", "dquery")}
        raw["gout"] = tile("gout_raw", [P, PACK, Q], F32, tag="gout_raw_then_p")
        grouped = {n: tile(n + "_grouped", [P, Q, PACK], BF16) for n in rows}
        codes = {n: tile(n + "_codes", [P, Q], U32) for n in rows}
        code_scales = {n: tile(n + "_code_scales", [P, Q], U8) for n in rows}
        window = tile("window", [P, T], F32)
        size_cols = tile("size_cols", [P, SIZES_A_PARTITION], F32)
        ident = tile("ident", [P, P], F32)
        minus_one = tile("minus_one", [P, 1], F32)
        warm = tile("warm", [P, 1], F32)

        def load_words(name, src):
            nc.sync.dma_start(out=pool_words[name][:].bitcast(I32), in_=src[0].bitcast(I32))

        def load_rows(name):
            nc.sync.dma_start(out=raw[name][:], in_=rows[name].rearrange("(p t) q -> p t q", t=PACK))

        def group(name):
            nc.scalar.copy(
                out=grouped[name][:].rearrange("p (c i) t -> p c t i", i=LINE),
                in_=raw[name][:].rearrange("p t (c i) -> p c t i", i=LINE),
            )

        def quantize(name):
            nc.vector.quantize_mx(
                out=codes[name][:].bitcast(FP8X4),
                scales=code_scales[name][:],
                in_=grouped[name][:].rearrange("p c t -> p (c t)"),
            )

        def gather(listed, pool):
            nc.vector.tensor_copy(listed[:], pool[:].indirect(offsets[:]))

        def product(name, pool_name):
            bank = ps.tile([P, I], F32, name=name + "_bank")
            nc.tensor.matmul_mx(
                out=bank[:],
                lhsT=codes[name][:].bitcast(FP8X4),
                lhsT_scale=code_scales[name][:],
                rhs=listed_words[pool_name][:].bitcast(FP4X4),
                rhs_scale=listed_scales[pool_name][:],
                start=True,
                stop=True,
            )
            return bank

        nc.vector.memset(warm[:], 0.0)
        nc.gpsimd.memset(pool_scales["vals"][:].bitcast(I32), 0)
        make_identity(nc, ident[:])
        nc.gpsimd.memset(minus_one[:], -1.0)
        nc.vector.memset(window[:], 0.0)

        nc.sync.dma_start(offsets[:], offs)
        for q in range(QUADRANTS):
            nc.sync.dma_start(
                out=pool_scales["keys"][QUADRANT * q : QUADRANT * (q + 1), :].bitcast(I32),
                in_=keys_scales[0:1, SCALE_ROWS * q : SCALE_ROWS * (q + 1), :]
                .bitcast(I32)
                .broadcast_to([QUADRANT // SCALE_ROWS, SCALE_ROWS, T // 4]),
            )
        load_words("keys", keys_words)
        load_rows("query2")
        load_rows("query")
        nc.scalar.activation(out=warm[:], in_=warm[:], func=ACT.Exp)
        load_rows("dquery")
        load_words("vals", vals_words)
        load_rows("gout")
        nc.sync.dma_start(out=size_cols[:], in_=size.rearrange("o (p j) -> (o p) j", j=SIZES_A_PARTITION))
        for q in range(QUADRANTS):
            nc.sync.dma_start(
                out=pool_scales["vals"][QUADRANT * q : QUADRANT * q + SCALE_ROWS, :].bitcast(I32),
                in_=vals_scales[0, SCALE_ROWS * q : SCALE_ROWS * (q + 1), :].bitcast(I32),
            )

        gather(listed_scales["keys"], pool_scales["keys"])
        gather(listed_words["keys"], pool_words["keys"])
        group("query2")
        quantize("query2")
        b_bank = product("query2", "keys")
        group("query")
        quantize("query")
        a_bank = product("query", "keys")
        group("dquery")
        quantize("dquery")
        ta_bank = product("dquery", "keys")

        base_sb = tile("base_sb", [P, T], F32, tag="keys_scales_then_base")
        nc.sync.dma_start(out=base_sb[:], in_=base)

        u = tile("u", [P, I], F32)
        nc.scalar.activation(out=u[:], in_=b_bank[:], func=ACT.Copy, bias=1.0)

        ta = tile("ta", [P, I], F32)
        ts = tile("ts", [P, I], F32)
        nc.scalar.copy(out=ta[:], in_=ta_bank[:])
        nc.gpsimd.tensor_tensor(ts[:], ta[:], u[:], ALU.mult)
        group("gout")

        s = tile("s", [P, I], F32, tag="s_then_size_all")
        nc.vector.tensor_tensor(s[:], a_bank[:], u[:], ALU.mult)
        gather(listed_words["vals"], pool_words["vals"])
        quantize("gout")
        neg_max = tile("neg_max", [P, 1], F32, tag="vals_words_then_neg_max")
        nc.vector.tensor_reduce(neg_max[:], s[:], mybir.AxisListType.X, ALU.max, negate=True)
        p = tile("p", [P, I], F32, tag="gout_raw_then_p")
        z = tile("z", [P, 1], F32)
        nc.scalar.activation(out=p[:], in_=s[:], func=ACT.Exp, bias=neg_max[:], accum_out=z[:])
        gather(listed_scales["vals"], pool_scales["vals"])
        c0_bank = product("gout", "vals")

        size_bank = ps.tile([P, SIZES_A_PARTITION, P], F32, name="size_bank")
        for j in range(SIZES_A_PARTITION):
            nc.tensor.transpose(size_bank[:, j, :], size_cols[:, j : j + 1].to_broadcast([P, P]), ident[:])
        size_all = tile("size_all", [P, P, SIZES_A_PARTITION], F32, tag="s_then_size_all")
        nc.scalar.activation(
            out=size_all[:], in_=size_bank[:].rearrange("m j n -> m n j"), func=ACT.Copy, scale=-OUT_SCALE
        )

        r = tile("r", [P, 1], F32)
        nc.gpsimd.tensor_tensor(r[:], z[:], minus_one[:], ALU.pow)

        ts_mean = tile("ts_mean", [P, 1], F32)
        c_mean = tile("c_mean", [P, 1], F32)
        y_sum = tile("y_sum", [P, 1], F32)
        v = tile("v", [P, I], F32, tag="vals_scales_then_v")
        nc.vector.scalar_tensor_tensor(v[:], ts[:], r[:], p[:], ALU.mult, ALU.mult, accum_out=ts_mean[:])
        c = tile("c", [P, I], F32)
        nc.vector.tensor_tensor(c[:], c0_bank[:], size_all[:].rearrange("m n j -> m (n j)"), ALU.mult)
        nc.vector.scalar_tensor_tensor(v[:], ts[:], ts_mean[:], p[:], ALU.subtract, ALU.mult)
        y = tile("y", [P, I], F32)
        nc.vector.scalar_tensor_tensor(y[:], c[:], r[:], p[:], ALU.mult, ALU.mult, accum_out=c_mean[:])
        nc.vector.scalar_tensor_tensor(y[:], c[:], c_mean[:], v[:], ALU.subtract, ALU.mult, accum_out=y_sum[:])

        pr = tile("pr", [P, I], F32)
        ur = tile("ur", [P, I], F32)
        nc.scalar.activation(out=pr[:], in_=p[:], func=ACT.Copy, scale=r[:])
        nc.scalar.activation(out=ur[:], in_=u[:], func=ACT.Copy, scale=r[:])
        centred = tile("centred", [P, I], F32)
        nc.vector.scalar_tensor_tensor(centred[:], pr[:], y_sum[:], y[:], ALU.mult, ALU.subtract)
        nc.vector.tensor_tensor(window[:].indirect(offsets[:]), centred[:], ur[:], ALU.mult)

        first = 0
        for n, width in enumerate(OUT_PIECES):
            cols = slice(first, first + width)
            piece = tile("piece%d" % n, [P, width], F32)
            nc.vector.tensor_tensor(piece[:], window[:, cols], base_sb[:, cols], ALU.add)
            nc.sync.dma_start(out=out[:, cols], in_=piece[:])
            first += width
